import numpy as np
import ml_dtypes


def mxq(x, axis, fmt="e4m3"):
    dtype, down = {"e4m3": (ml_dtypes.float8_e4m3fn, 7), "e5m2": (ml_dtypes.float8_e5m2, 14)}[fmt]
    v = np.moveaxis(np.asarray(x, np.float32).astype(ml_dtypes.bfloat16).astype(np.float64), axis, -1)
    blocks = v.reshape(v.shape[:-1] + (-1, 32))
    amax = np.abs(blocks).max(-1, keepdims=True)
    byte = np.maximum(np.where(amax > 0, np.frexp(amax)[1] - 1 + 127, 0) - down, 1)
    scale = np.exp2(byte - 127.0)
    codes = (blocks / scale).astype(np.float32).astype(dtype).astype(np.float64)
    return np.moveaxis((codes * scale).reshape(v.shape), -1, axis)


WIDE = False


def mx_kscale(k):
    if not WIDE:
        return np.ones(k)
    levels = np.array([10, -10, 5, -5, 0])
    if k % 512:
        return np.exp2(np.random.permutation(np.resize(levels, k // 32))).repeat(32)
    a = np.empty((k // 512, 16))
    for p in range(k // 512):
        a[p, :8] = np.random.permutation(np.resize(levels, 8))
        for g in range(8):
            far = levels[np.abs(levels - a[p, g]) >= 10]
            a[p, g + 8] = far[np.random.randint(len(far))]
    return np.exp2(a.ravel()).repeat(32)


def f64(x):
    return np.asarray(x).astype(np.float64)


def striped(idx):
    return np.tile(np.asarray(idx).reshape(-1, 16).T, (8, 1)).astype(np.uint16)


def unstriped(offs):
    return offs[:16].T.reshape(-1).astype(np.int64)


def striped8(idx):
    return np.asarray(idx).reshape(8, -1, 16).transpose(0, 2, 1).reshape(128, -1).astype(np.uint16)


def unstriped8(offs):
    return offs.reshape(8, 16, -1).transpose(0, 2, 1).reshape(8, -1).astype(np.int64)


def pick8(x, idx, run):
    r = np.arange(len(x))
    return x[r[:, None], idx[r % (8 * run) // run]]


E2M1 = np.array([0.0, 0.5, 1.0, 1.5, 2.0, 3.0, 4.0, 6.0, -0.0, -0.5, -1.0, -1.5, -2.0, -3.0, -4.0, -6.0])


def pack_weight(w, fmt):
    k, n = w.shape
    w = f64(np.asarray(w, np.float32).astype(ml_dtypes.bfloat16)).reshape(k // 32, 32, n)
    amax = np.abs(w).max(1)
    if fmt == "e4m3":
        byte = np.frexp(amax)[1] - 1 + 127 - 7
    else:
        mant, ex = np.frexp(amax / 6.0)
        byte = np.where(mant > 0.5, ex, ex - 1) + 127
    byte = np.clip(np.where(amax > 0, byte, 1), 1, 254)
    scaled = (w * np.exp2(127.0 - byte)[:, None, :]).reshape(k, n).astype(np.float32)
    by_word = np.ascontiguousarray(scaled.reshape(k // 512, 128, 4, n).transpose(0, 1, 3, 2))
    if fmt == "e4m3":
        words = by_word.astype(ml_dtypes.float8_e4m3fn).view(np.uint8)
    else:
        c = by_word.astype(ml_dtypes.float4_e2m1fn).view(np.uint8) & 0xF
        words = (c[..., 0::2] | (c[..., 1::2] << 4)).reshape(k // 512, 128, 2 * n)
    return np.ascontiguousarray(words), np.ascontiguousarray(byte.astype(np.uint8).reshape(k // 512, 16, n))


def unpack_weight(words, scales, fmt):
    g, _, n = scales.shape
    words = np.ascontiguousarray(words).reshape(g, 128, n, -1)
    if fmt == "e4m3":
        vals = words.view(ml_dtypes.float8_e4m3fn).astype(np.float64)
    else:
        nib = np.empty((g, 128, n, 4), np.uint8)
        nib[..., 0::2] = words & 0xF
        nib[..., 1::2] = words >> 4
        vals = E2M1[nib]
    vals = vals * np.repeat(np.exp2(scales.astype(np.float64) - 127.0), 8, axis=1)[..., None]
    return vals.transpose(0, 1, 3, 2).reshape(g * 512, n)


K, J, R, T, Z, M, C, O, N, U = 512, 512, 512, 1024, 512, 1024, 1024, 512, 256, 1024


def setup_inputs():
    n = np.random.standard_normal
    idx = np.random.permutation(T)[:J]
    idx2 = np.random.permutation(M)[:J]
    idx3 = np.stack([np.random.permutation(C)[:J] for _ in range(8)])
    idx4 = np.stack([np.random.permutation(C)[:J] for _ in range(8)])
    idx5 = np.stack([np.random.permutation(C)[:O] for _ in range(8)])
    idx6 = np.stack([np.random.permutation(U)[:O] for _ in range(8)])
    idx7 = np.stack([np.random.permutation(U)[:O] for _ in range(8)])
    fk = mx_kscale(K)
    fz = mx_kscale(Z)
    fr = mx_kscale(R)
    xtp = pack_weight(n((K, T)) * fk[:, None], "e4m3")
    wp = pack_weight(n((K, R)) * 1 / np.sqrt(K) / fk[:, None], "e2m1")
    xop = pack_weight(n((Z, M)) / fz[:, None], "e2m1")
    w2p = pack_weight(n((Z, R)) * 1 / np.sqrt(Z) * fz[:, None], "e4m3")
    wbp = pack_weight(n((R, N)) * 1 / np.sqrt(R) / fr[:, None], "e4m3")
    return {
        "xt_words": xtp[0],
        "xt_scales": xtp[1],
        "w_words": wp[0],
        "w_scales": wp[1],
        "xo_words": xop[0],
        "xo_scales": xop[1],
        "w2_words": w2p[0],
        "w2_scales": w2p[1],
        "sa": (np.random.uniform(0.5, 1.6, (R, 1)) * fr[:, None]).astype(np.float32),
        "wb_words": wbp[0],
        "wb_scales": wbp[1],
        "offs": striped(idx),
        "offs2": striped(idx2),
        "offs3": striped8(idx3),
        "offs4": striped8(idx4),
        "offs5": striped8(idx5),
        "offs6": striped8(idx6),
        "offs7": striped8(idx7),
    }


def reference(xt_words, xt_scales, w_words, w_scales, xo_words, xo_scales, w2_words, w2_scales, sa, wb_words, wb_scales, offs, offs2, offs3, offs4, offs5, offs6, offs7):
    idx = unstriped(offs)
    idx2 = unstriped(offs2)
    idx3 = unstriped8(offs3)
    idx4 = unstriped8(offs4)
    idx5 = unstriped8(offs5)
    idx6 = unstriped8(offs6)
    idx7 = unstriped8(offs7)
    xtu = unpack_weight(xt_words, xt_scales, "e4m3")
    wu = unpack_weight(w_words, w_scales, "e2m1")
    xou = unpack_weight(xo_words, xo_scales, "e2m1")
    w2u = unpack_weight(w2_words, w2_scales, "e4m3")
    wbu = unpack_weight(wb_words, wb_scales, "e4m3")
    xtidxg = xtu[:, idx]
    a = wu.T @ xtidxg
    xoidx2g = xou[:, idx2]
    b = w2u.T @ xoidx2g
    pw = np.zeros((R, C))
    pw[np.arange(R)[:, None], idx3[np.arange(R) % 512 // 64]] = a
    pv = np.zeros((R, C))
    pv[np.arange(R)[:, None], idx4[np.arange(R) % 512 // 64]] = b
    pg = np.maximum(pw, pv)
    pm = np.mean(np.abs(pg), axis=1, keepdims=True)
    ql = f64(sa) / pm
    hid = pick8(pg, idx5, 64) * ql
    hidq = mxq(hid, 0, "e4m3")
    p = wbu.T @ hidq
    m0 = np.maximum(p, 0.0)
    m1 = np.maximum(-p, 0.0)
    m2 = np.zeros((N, U))
    m2[np.arange(N)[:, None], idx6[np.arange(N) % 128 // 16]] = m0
    m3 = np.zeros((N, U))
    m3[np.arange(N)[:, None], idx7[np.arange(N) % 128 // 16]] = m1
    y = m2 - m3
    return y

@@ -1,0 +1,265 @@
+from contextlib import ExitStack
+
+import concourse.mybir as mybir
+
+F32 = mybir.dt.float32
+BF16 = mybir.dt.bfloat16
+I32 = mybir.dt.int32
+U32 = mybir.dt.uint32
+U16 = mybir.dt.uint16
+U8 = mybir.dt.uint8
+FP8X4 = mybir.dt.float8_e4m3fn_x4
+FP4X4 = mybir.dt.float4_e2m1fn_x4
+ALU = mybir.AluOpType
+COPY = mybir.ActivationFunctionType.Copy
+AXIS_X = mybir.AxisListType.X
+
+P = 128
+PACK = 4
+J, R, T, C, O, N, U = 512, 512, 1024, 1024, 512, 256, 1024
+GROUP = 16
+FLOPS = 2 * 512 * 512 * 512 * 2 + 2 * 512 * 256 * 512
+
+FIRST = 128
+
+
+def tile_picked_tokens_bare_two_levelled_one_endsplit_kernel(
+    tc, xt_words, xt_scales, w_words, w_scales, xo_words, xo_scales, w2_words, w2_scales,
+    sa, wb_words, wb_scales, offs, offs2, offs3, offs4, offs5, offs6, offs7, out,
+):
+    nc = tc.nc
+    with ExitStack() as ctx:
+        lists = ctx.enter_context(tc.tile_pool(name="lists", bufs=1))
+        sb = ctx.enter_context(tc.tile_pool(name="sb", bufs=1))
+        psum = ctx.enter_context(tc.psum_pool(name="psum", bufs=8))
+
+        def tile(name, shape, dtype, tag=None):
+            return sb.tile(shape, dtype, name=name, tag=tag or name, align_bytes=64)
+
+        def load_list(name, src):
+            t = lists.tile([P, J // GROUP], U16, name=name)
+            nc.sync.dma_start(t[:], src)
+            return t
+
+        def part(lst, a, b):
+            return lst[:, a // GROUP : b // GROUP]
+
+        def zeroed_plane(name, width):
+            t = tile(name, [P, width], U8)
+            nc.vector.memset(t[:].bitcast(I32), 0)
+            return t
+
+        def load_plane(plane, src):
+            for q in range(4):
+                nc.sync.dma_start(plane[32 * q : 32 * q + 4, :].bitcast(I32), src[0, 4 * q : 4 * q + 4, :].bitcast(I32))
+
+        def load_stage(name, src, width):
+            t = tile(name, [4, 4, width // 4], I32)
+            nc.sync.dma_start(t[:], src[0].bitcast(I32).rearrange("(q r) w -> r q w", q=4))
+            return t
+
+        def spread(plane, stage):
+            for q in range(4):
+                nc.vector.tensor_copy(out=plane[32 * q : 32 * q + 4, :].bitcast(I32), in_=stage[:, q, :])
+
+        def load_words(name, src, width, dtype):
+            t = tile(name, [P, width], dtype)
+            nc.sync.dma_start(t[:].bitcast(I32), src.bitcast(I32))
+            return t
+
+        def board(name, tag=None):
+            t = tile(name, [P, C], F32, tag)
+            nc.vector.memset(t[:].bitcast(I32), 0)
+            return t
+
+        def product(lhs, lhs_scale, rhs, rhs_scale, acc):
+            nc.tensor.matmul_mx(out=acc, lhsT=lhs, lhsT_scale=lhs_scale, rhs=rhs, rhs_scale=rhs_scale, start=True, stop=True)
+
+        def scatter(window, lst, values, a, b):
+            nc.scalar.activation(out=window[:].indirect(part(lst, a, b)), in_=values[:, a:b], func=COPY)
+
+        xo_plane = zeroed_plane("xo_plane", T)
+        w2_plane = zeroed_plane("w2_plane", R)
+        l_xo = load_list("l_xo", offs2)
+        xo_win = load_words("xo_win", xo_words[0], T, U16)
+        load_plane(xo_plane, xo_scales)
+        w2_stage = load_stage("w2_stage", w2_scales, R)
+        w2_raw = load_words("w2_raw", w2_words[0].rearrange("p n t -> p (n t)"), R, U32)
+        l_pv = load_list("l_pv", offs4)
+        pv = [board("pv%d" % t) for t in range(PACK)]
+
+        xt_plane = zeroed_plane("xt_plane", T)
+        w_plane = zeroed_plane("w_plane", R)
+        wb_plane = zeroed_plane("wb_plane", N)
+        l_xt = load_list("l_xt", offs)
+        xt_win = load_words("xt_win", xt_words[0].rearrange("p n t -> p (n t)"), T, U32)
+        load_plane(xt_plane, xt_scales)
+        w_raw = load_words("w_raw", w_words[0], 2 * R, U8)
+        load_plane(w_plane, w_scales)
+        l_pw = load_list("l_pw", offs3)
+        sa_sb = tile("sa_sb", [P, PACK], F32)
+        nc.sync.dma_start(sa_sb[:], sa.rearrange("(p t) o -> p (t o)", t=PACK))
+        l_hid = load_list("l_hid", offs5)
+        wb = load_words("wb", wb_words[0].rearrange("p n t -> p (n t)"), N, U32)
+        load_plane(wb_plane, wb_scales)
+        l_m2 = load_list("l_m2", offs6)
+        l_m3 = load_list("l_m3", offs7)
+
+        spread(w2_plane, w2_stage)
+        w2_sc = tile("w2_sc", [P, PACK, P], U8)
+        w2_d = tile("w2_d", [P, PACK, P], U32)
+        b_sb = [tile("b_sb%d" % t, [P, J], F32) for t in range(PACK)]
+
+        def deal_w2(t0, t1):
+            nc.vector.tensor_copy(out=w2_sc[:, t0:t1, :], in_=w2_plane[:].rearrange("p (m t) -> p t m", t=PACK)[:, t0:t1, :])
+            nc.vector.tensor_copy(
+                out=w2_d[:, t0:t1, :].rearrange("p t m -> p m t"),
+                in_=w2_raw[:].rearrange("p (m t) -> p m t", t=PACK)[:, :, t0:t1],
+            )
+
+        def gather_notes(a, b):
+            words = tile("xo_g%d" % a, [P, b - a], U16, "xo_g")
+            scales = tile("xo_gs%d" % a, [P, b - a], U8, "xo_gs")
+            nc.vector.tensor_copy(out=words[:], in_=xo_win[:].indirect(part(l_xo, a, b)))
+            nc.vector.tensor_copy(out=scales[:], in_=xo_plane[:].indirect(part(l_xo, a, b)))
+            return words, scales
+
+        def make_b(t, words, scales, cuts):
+            acc = psum.tile([P, J], F32, name="acc")
+            a, b = cuts[0], cuts[-1]
+            for c, d in zip(cuts, cuts[1:]):
+                cols = slice(c - a, d - a)
+                product(w2_d[:, t, :].bitcast(FP8X4), w2_sc[:, t, :], words[:, cols].bitcast(FP4X4), scales[:, cols], acc[:, c:d])
+            if (t, a) == (0, 0):
+                nc.scalar.activation(out=b_sb[t][:, a:b], in_=acc[:, a:b], func=COPY)
+            else:
+                nc.vector.tensor_copy(out=b_sb[t][:, a:b], in_=acc[:, a:b])
+            scatter(pv[t], l_pv, b_sb[t], a, b)
+
+        deal_w2(0, 1)
+        words, scales = gather_notes(0, FIRST)
+        make_b(0, words, scales, (0, FIRST))
+        deal_w2(1, PACK)
+        for t in range(1, PACK):
+            make_b(t, words, scales, (0, FIRST))
+        for a, b in ((FIRST, J // 2), (J // 2, J)):
+            words, scales = gather_notes(a, b)
+            for t in range(PACK):
+                make_b(t, words, scales, (a, b))
+
+        xt_g = tile("xt_g", [P, J], U32, "xo_win")
+        xt_gs = tile("xt_gs", [P, J], U8, "xo_plane")
+        nc.vector.tensor_copy(out=xt_g[:], in_=xt_win[:].indirect(l_xt[:]))
+        nc.vector.tensor_copy(out=xt_gs[:], in_=xt_plane[:].indirect(l_xt[:]))
+        w_sc = tile("w_sc", [P, PACK, P], U8, "w2_sc")
+        w_d = tile("w_d", [P, PACK, 2 * P], U8, "w2_d")
+        nc.vector.tensor_copy(out=w_sc[:], in_=w_plane[:].rearrange("p (m t) -> p t m", t=PACK))
+        nc.vector.tensor_copy(
+            out=w_d[:].rearrange("p t (m e) -> p t m e", e=2),
+            in_=w_raw[:].rearrange("p (m t e) -> p t m e", t=PACK, e=2),
+        )
+        a_sb = [tile("a_sb%d" % t, [P, J], F32) for t in range(PACK)]
+
+        def make_a(t):
+            acc = psum.tile([P, J], F32, name="acc")
+            product(w_d[:, t, :].bitcast(FP4X4), w_sc[:, t, :], xt_g[:].bitcast(FP8X4), xt_gs[:], acc[:])
+            nc.vector.tensor_copy(out=a_sb[t][:], in_=acc[:])
+
+        pw = [board("pw0", "xo_g")]
+        make_a(0)
+        pw.append(board("pw1", "xo_gs"))
+        make_a(1)
+        make_a(2)
+        make_a(3)
+        m2 = [board("m2_0", "xt_plane"), board("m2_1", "w_plane")]
+        m3 = [board("m3_0", "w_raw"), board("m3_1", "xt_win")]
+
+        pg = [tile("pg%d" % t, [P, C], F32) for t in range(PACK)]
+        total = tile("total", [P, PACK], F32)
+        recip = tile("recip", [P, PACK], F32)
+        level = tile("level", [P, PACK], F32)
+
+        late = tile("late", [P, PACK], F32)
+
+        def make_level(dst, cols):
+            nc.vector.scalar_tensor_tensor(
+                out=dst[:, cols], in0=recip[:, cols], scalar=float(C), in1=sa_sb[:, cols], op0=ALU.mult, op1=ALU.mult
+            )
+
+        def join(t):
+            col = slice(t, t + 1)
+            nc.vector.tensor_tensor(out=pg[t][:], in0=pw[t % 2][:], in1=pv[t][:], op=ALU.max)
+            nc.vector.tensor_reduce(out=total[:, col], in_=pg[t][:], axis=AXIS_X, op=ALU.add, apply_absolute_value=True)
+            nc.vector.reciprocal(out=recip[:, col], in_=total[:, col])
+
+        for t in range(PACK):
+            scatter(pw[t % 2], l_pw, a_sb[t], 0, J)
+            join(t)
+            if t < PACK - 1:
+                make_level(level, slice(t, t + 1))
+        make_level(late, slice(1, PACK))
+
+        planes = tile("planes", [P, PACK, O], BF16, "a_sb3")
+
+        def fetch(t, half, levels):
+            a, b = half * O // 2, (half + 1) * O // 2
+            nc.scalar.activation(
+                out=planes[:, t, a:b], in_=pg[t][:].indirect(part(l_hid, a, b)), func=COPY, scale=levels[:, t : t + 1]
+            )
+
+        for t in range(PACK - 1):
+            fetch(t, 0, level)
+        fetch(0, 1, level)
+        fetch(PACK - 1, 0, late)
+        for t in range(1, PACK):
+            fetch(t, 1, late)
+
+        m0 = [tile("m0_%d" % n, [P, O], F32) for n in range(2)]
+        m1 = [tile("m1_%d" % n, [P, O], F32) for n in range(2)]
+
+        def weave(a, b, tag=None):
+            woven = tile("woven%d" % a, [P, b - a, PACK], BF16, tag)
+            nc.vector.tensor_copy(
+                out=woven[:].rearrange("p (c i) t -> p c t i", i=4),
+                in_=planes[:, :, a:b].rearrange("p t (c i) -> p c t i", i=4),
+            )
+            return woven
+
+        def quantise(woven, a, b):
+            words = tile("hid_q%d" % a, [P, b - a], U32)
+            scales = tile("hid_s%d" % a, [P, b - a], U8)
+            nc.vector.quantize_mx(out=words[:].bitcast(FP8X4), scales=scales[:], in_=woven[:].rearrange("p c t -> p (c t)"))
+            return words, scales
+
+        def make_p(n, words, scales, cuts):
+            acc = psum.tile([P, O], F32, name="acc")
+            rows = slice(n * P, (n + 1) * P)
+            for c, d in zip(cuts, cuts[1:]):
+                cols = slice(c - cuts[0], d - cuts[0])
+                product(wb[:, rows].bitcast(FP8X4), wb_plane[:, rows], words[:, cols].bitcast(FP8X4), scales[:, cols], acc[:, c:d])
+            return acc
+
+        def split(n, acc, a, b):
+            nc.vector.tensor_scalar(out=m0[n][:, a:b], in0=acc[:, a:b], scalar1=0.0, scalar2=None, op0=ALU.max)
+            scatter(m2[n], l_m2, m0[n], a, b)
+            nc.vector.tensor_scalar(out=m1[n][:, a:b], in0=acc[:, a:b], scalar1=-1.0, scalar2=0.0, op0=ALU.mult, op1=ALU.max)
+            scatter(m3[n], l_m3, m1[n], a, b)
+
+        def store(n, pieces):
+            res = tile("res%d" % n, [P, U], F32)
+            width = U // pieces
+            for u in range(0, U, width):
+                cols = slice(u, u + width)
+                nc.vector.tensor_tensor(out=res[:, cols], in0=m2[n][:, cols], in1=m3[n][:, cols], op=ALU.subtract)
+                nc.sync.dma_start(out[n * P : (n + 1) * P, cols], res[:, cols])
+
+        words, scales = quantise(weave(0, FIRST), 0, FIRST)
+        accs = [make_p(n, words, scales, (0, FIRST)) for n in range(2)]
+        split(0, accs[0], 0, FIRST)
+        woven = weave(FIRST, O, "hid_q0")
+        split(1, accs[1], 0, FIRST)
+        words, scales = quantise(woven, FIRST, O)
+        for n in range(2):
+            split(n, make_p(n, words, scales, (FIRST, O // 2, O)), FIRST, O)
+        store(0, 2)
+        store(1, 4)

@@ -46,7 +46,7 @@ def tile_picked_tokens_bare_two_levelled_one_endsplit_kernel(
 
         def zeroed_plane(name, width):
             t = tile(name, [P, width], U8)
-            nc.vector.memset(t[:].bitcast(I32), 0)
+            nc.gpsimd.memset(t[:].bitcast(I32), 0)
             return t
 
         def load_plane(plane, src):
@@ -69,7 +69,7 @@ def tile_picked_tokens_bare_two_levelled_one_endsplit_kernel(
 
         def board(name, tag=None):
             t = tile(name, [P, C], F32, tag)
-            nc.vector.memset(t[:].bitcast(I32), 0)
+            (nc.gpsimd if tag else nc.vector).memset(t[:], 0.0)
             return t
 
         def product(lhs, lhs_scale, rhs, rhs_scale, acc):
@@ -80,17 +80,15 @@ def tile_picked_tokens_bare_two_levelled_one_endsplit_kernel(
 
         xo_plane = zeroed_plane("xo_plane", T)
         w2_plane = zeroed_plane("w2_plane", R)
-        l_xo = load_list("l_xo", offs2)
-        xo_win = load_words("xo_win", xo_words[0], T, U16)
-        load_plane(xo_plane, xo_scales)
-        w2_stage = load_stage("w2_stage", w2_scales, R)
-        w2_raw = load_words("w2_raw", w2_words[0].rearrange("p n t -> p (n t)"), R, U32)
-        l_pv = load_list("l_pv", offs4)
-        pv = [board("pv%d" % t) for t in range(PACK)]
-
         xt_plane = zeroed_plane("xt_plane", T)
         w_plane = zeroed_plane("w_plane", R)
         wb_plane = zeroed_plane("wb_plane", N)
+        w2_stage = load_stage("w2_stage", w2_scales, R)
+        l_xo = load_list("l_xo", offs2)
+        load_plane(xo_plane, xo_scales)
+        xo_win = load_words("xo_win", xo_words[0], T, U16)
+        w2_raw = load_words("w2_raw", w2_words[0].rearrange("p n t -> p (n t)"), R, U32)
+        l_pv = load_list("l_pv", offs4)
         l_xt = load_list("l_xt", offs)
         xt_win = load_words("xt_win", xt_words[0].rearrange("p n t -> p (n t)"), T, U32)
         load_plane(xt_plane, xt_scales)
@@ -105,13 +103,15 @@ def tile_picked_tokens_bare_two_levelled_one_endsplit_kernel(
         l_m2 = load_list("l_m2", offs6)
         l_m3 = load_list("l_m3", offs7)
 
-        spread(w2_plane, w2_stage)
         w2_sc = tile("w2_sc", [P, PACK, P], U8)
         w2_d = tile("w2_d", [P, PACK, P], U32)
         b_sb = [tile("b_sb%d" % t, [P, J], F32) for t in range(PACK)]
+        pv = [board("pv0")]
+        spread(w2_plane, w2_stage)
+        nc.vector.tensor_copy(out=w2_sc[:], in_=w2_plane[:].rearrange("p (m t) -> p t m", t=PACK))
+        pv.extend(board("pv%d" % t) for t in range(1, PACK))
 
         def deal_w2(t0, t1):
-            nc.vector.tensor_copy(out=w2_sc[:, t0:t1, :], in_=w2_plane[:].rearrange("p (m t) -> p t m", t=PACK)[:, t0:t1, :])
             nc.vector.tensor_copy(
                 out=w2_d[:, t0:t1, :].rearrange("p t m -> p m t"),
                 in_=w2_raw[:].rearrange("p (m t) -> p m t", t=PACK)[:, :, t0:t1],
@@ -120,8 +120,8 @@ def tile_picked_tokens_bare_two_levelled_one_endsplit_kernel(
         def gather_notes(a, b):
             words = tile("xo_g%d" % a, [P, b - a], U16, "xo_g")
             scales = tile("xo_gs%d" % a, [P, b - a], U8, "xo_gs")
-            nc.vector.tensor_copy(out=words[:], in_=xo_win[:].indirect(part(l_xo, a, b)))
             nc.vector.tensor_copy(out=scales[:], in_=xo_plane[:].indirect(part(l_xo, a, b)))
+            nc.vector.tensor_copy(out=words[:], in_=xo_win[:].indirect(part(l_xo, a, b)))
             return words, scales
 
         def make_b(t, words, scales, cuts):
@@ -136,8 +136,8 @@ def tile_picked_tokens_bare_two_levelled_one_endsplit_kernel(
                 nc.vector.tensor_copy(out=b_sb[t][:, a:b], in_=acc[:, a:b])
             scatter(pv[t], l_pv, b_sb[t], a, b)
 
-        deal_w2(0, 1)
         words, scales = gather_notes(0, FIRST)
+        deal_w2(0, 1)
         make_b(0, words, scales, (0, FIRST))
         deal_w2(1, PACK)
         for t in range(1, PACK):
@@ -174,37 +174,41 @@ def tile_picked_tokens_bare_two_levelled_one_endsplit_kernel(
         m2 = [board("m2_0", "xt_plane"), board("m2_1", "w_plane")]
         m3 = [board("m3_0", "w_raw"), board("m3_1", "xt_win")]
 
-        pg = [tile("pg%d" % t, [P, C], F32) for t in range(PACK)]
-        total = tile("total", [P, PACK], F32)
-        recip = tile("recip", [P, PACK], F32)
+        inv_sa = tile("inv_sa", [P, PACK], F32, "w2_sc")
+        nc.vector.reciprocal(out=inv_sa[:], in_=sa_sb[:])
+        inv_weight = tile("inv_weight", [P, PACK], F32)
+        nc.vector.tensor_scalar(out=inv_weight[:], in0=inv_sa[:], scalar1=1.0 / C, scalar2=None, op0=ALU.mult)
+        pg = []
+        inv_level = tile("inv_level", [P, PACK], F32)
         level = tile("level", [P, PACK], F32)
-
         late = tile("late", [P, PACK], F32)
-
-        def make_level(dst, cols):
-            nc.vector.scalar_tensor_tensor(
-                out=dst[:, cols], in0=recip[:, cols], scalar=float(C), in1=sa_sb[:, cols], op0=ALU.mult, op1=ALU.mult
-            )
-
-        def join(t):
-            col = slice(t, t + 1)
-            nc.vector.tensor_tensor(out=pg[t][:], in0=pw[t % 2][:], in1=pv[t][:], op=ALU.max)
-            nc.vector.tensor_reduce(out=total[:, col], in_=pg[t][:], axis=AXIS_X, op=ALU.add, apply_absolute_value=True)
-            nc.vector.reciprocal(out=recip[:, col], in_=total[:, col])
+        halves = (slice(0, C // 2), slice(C // 2, C))
 
         for t in range(PACK):
+            col = slice(t, t + 1)
             scatter(pw[t % 2], l_pw, a_sb[t], 0, J)
-            join(t)
+            pg.append(tile("pg%d" % t, [P, C], F32, "sums%d" % (t - 1) if t else None))
+            for cols in halves:
+                nc.vector.tensor_tensor(out=pg[t][:, cols], in0=pw[t % 2][:, cols], in1=pv[t][:, cols], op=ALU.max)
+            sums = tile("sums%d" % t, [P, 2], F32)
+            for h, cols in enumerate(halves):
+                nc.vector.tensor_reduce(
+                    out=sums[:, h : h + 1], in_=pg[t][:, cols], axis=AXIS_X, op=ALU.add, apply_absolute_value=True
+                )
+            nc.vector.tensor_scalar(
+                out=inv_level[:, col], in0=sums[:, 0:1], scalar1=sums[:, 1:2], scalar2=inv_weight[:, col],
+                op0=ALU.add, op1=ALU.mult,
+            )
             if t < PACK - 1:
-                make_level(level, slice(t, t + 1))
-        make_level(late, slice(1, PACK))
+                nc.vector.reciprocal(out=level[:, col], in_=inv_level[:, col])
+        nc.vector.reciprocal(out=late[:, 1:], in_=inv_level[:, 1:])
 
-        planes = tile("planes", [P, PACK, O], BF16, "a_sb3")
+        planes = [tile("planes0", [P, PACK, O // 2], BF16, "a_sb3"), tile("planes1", [P, PACK, O // 2], BF16, "xo_g")]
 
         def fetch(t, half, levels):
             a, b = half * O // 2, (half + 1) * O // 2
             nc.scalar.activation(
-                out=planes[:, t, a:b], in_=pg[t][:].indirect(part(l_hid, a, b)), func=COPY, scale=levels[:, t : t + 1]
+                out=planes[half][:, t, :], in_=pg[t][:].indirect(part(l_hid, a, b)), func=COPY, scale=levels[:, t : t + 1]
             )
 
         for t in range(PACK - 1):
@@ -217,13 +221,10 @@ def tile_picked_tokens_bare_two_levelled_one_endsplit_kernel(
         m0 = [tile("m0_%d" % n, [P, O], F32) for n in range(2)]
         m1 = [tile("m1_%d" % n, [P, O], F32) for n in range(2)]
 
-        def weave(a, b, tag=None):
-            woven = tile("woven%d" % a, [P, b - a, PACK], BF16, tag)
+        def weave(dst, src):
             nc.vector.tensor_copy(
-                out=woven[:].rearrange("p (c i) t -> p c t i", i=4),
-                in_=planes[:, :, a:b].rearrange("p t (c i) -> p c t i", i=4),
+                out=dst.rearrange("p (c i) t -> p c t i", i=4), in_=src.rearrange("p t (c i) -> p c t i", i=4)
             )
-            return woven
 
         def quantise(woven, a, b):
             words = tile("hid_q%d" % a, [P, b - a], U32)
@@ -253,13 +254,14 @@ def tile_picked_tokens_bare_two_levelled_one_endsplit_kernel(
                 nc.vector.tensor_tensor(out=res[:, cols], in0=m2[n][:, cols], in1=m3[n][:, cols], op=ALU.subtract)
                 nc.sync.dma_start(out[n * P : (n + 1) * P, cols], res[:, cols])
 
-        words, scales = quantise(weave(0, FIRST), 0, FIRST)
-        accs = [make_p(n, words, scales, (0, FIRST)) for n in range(2)]
-        split(0, accs[0], 0, FIRST)
-        woven = weave(FIRST, O, "hid_q0")
-        split(1, accs[1], 0, FIRST)
-        words, scales = quantise(woven, FIRST, O)
-        for n in range(2):
-            split(n, make_p(n, words, scales, (FIRST, O // 2, O)), FIRST, O)
+        held_by = None
+        for a, b in ((0, FIRST), (FIRST, O // 2), (O // 2, O)):
+            half, start = divmod(a, O // 2)
+            woven = tile("woven%d" % a, [P, b - a, PACK], BF16, held_by)
+            weave(woven[:], planes[half][:, :, start : start + b - a])
+            words, scales = quantise(woven, a, b)
+            held_by = "hid_q%d" % a
+            for n in range(2):
+                split(n, make_p(n, words, scales, (a, b)), a, b)
         store(0, 2)
         store(1, 4)

@@ -67,9 +67,9 @@ def tile_picked_tokens_bare_two_levelled_one_endsplit_kernel(
             nc.sync.dma_start(t[:].bitcast(I32), src.bitcast(I32))
             return t
 
-        def board(name, tag=None):
+        def board(name, tag=None, engine=nc.vector):
             t = tile(name, [P, C], F32, tag)
-            (nc.gpsimd if tag else nc.vector).memset(t[:], 0.0)
+            engine.memset(t[:], 0.0)
             return t
 
         def product(lhs, lhs_scale, rhs, rhs_scale, acc):
@@ -153,11 +153,11 @@ def tile_picked_tokens_bare_two_levelled_one_endsplit_kernel(
         nc.vector.tensor_copy(out=xt_gs[:], in_=xt_plane[:].indirect(l_xt[:]))
         w_sc = tile("w_sc", [P, PACK, P], U8, "w2_sc")
         w_d = tile("w_d", [P, PACK, 2 * P], U8, "w2_d")
-        nc.vector.tensor_copy(out=w_sc[:], in_=w_plane[:].rearrange("p (m t) -> p t m", t=PACK))
         nc.vector.tensor_copy(
             out=w_d[:].rearrange("p t (m e) -> p t m e", e=2),
             in_=w_raw[:].rearrange("p (m t e) -> p t m e", t=PACK, e=2),
         )
+        nc.vector.tensor_copy(out=w_sc[:], in_=w_plane[:].rearrange("p (m t) -> p t m", t=PACK))
         a_sb = [tile("a_sb%d" % t, [P, J], F32) for t in range(PACK)]
 
         def make_a(t):
@@ -165,17 +165,16 @@ def tile_picked_tokens_bare_two_levelled_one_endsplit_kernel(
             product(w_d[:, t, :].bitcast(FP4X4), w_sc[:, t, :], xt_g[:].bitcast(FP8X4), xt_gs[:], acc[:])
             nc.vector.tensor_copy(out=a_sb[t][:], in_=acc[:])
 
-        pw = [board("pw0", "xo_g")]
+        pw = [board("pw0", "w2_raw")]
         make_a(0)
-        pw.append(board("pw1", "xo_gs"))
+        pw.append(board("pw1", "w_plane", nc.gpsimd))
         make_a(1)
         make_a(2)
         make_a(3)
-        m2 = [board("m2_0", "xt_plane"), board("m2_1", "w_plane")]
-        m3 = [board("m3_0", "w_raw"), board("m3_1", "xt_win")]
-
-        inv_sa = tile("inv_sa", [P, PACK], F32, "w2_sc")
+        inv_sa = tile("inv_sa", [P, PACK], F32, "xt_plane")
         nc.vector.reciprocal(out=inv_sa[:], in_=sa_sb[:])
+        m2 = [board("m2_0", "xo_win", nc.gpsimd), board("m2_1", "xo_plane", nc.gpsimd)]
+        m3 = [board("m3_0", "w2_d", nc.gpsimd), board("m3_1", "w2_sc", nc.gpsimd)]
         inv_weight = tile("inv_weight", [P, PACK], F32)
         nc.vector.tensor_scalar(out=inv_weight[:], in0=inv_sa[:], scalar1=1.0 / C, scalar2=None, op0=ALU.mult)
         pg = []
@@ -203,7 +202,7 @@ def tile_picked_tokens_bare_two_levelled_one_endsplit_kernel(
                 nc.vector.reciprocal(out=level[:, col], in_=inv_level[:, col])
         nc.vector.reciprocal(out=late[:, 1:], in_=inv_level[:, 1:])
 
-        planes = [tile("planes0", [P, PACK, O // 2], BF16, "a_sb3"), tile("planes1", [P, PACK, O // 2], BF16, "xo_g")]
+        planes = [tile("planes0", [P, PACK, O // 2], BF16, "a_sb3"), tile("planes1", [P, PACK, O // 2], BF16, "w2_raw")]
 
         def fetch(t, half, levels):
             a, b = half * O // 2, (half + 1) * O // 2

@@ -85,8 +85,8 @@ def tile_picked_tokens_bare_two_levelled_one_endsplit_kernel(
         wb_plane = zeroed_plane("wb_plane", N)
         w2_stage = load_stage("w2_stage", w2_scales, R)
         l_xo = load_list("l_xo", offs2)
-        load_plane(xo_plane, xo_scales)
         xo_win = load_words("xo_win", xo_words[0], T, U16)
+        load_plane(xo_plane, xo_scales)
         w2_raw = load_words("w2_raw", w2_words[0].rearrange("p n t -> p (n t)"), R, U32)
         l_pv = load_list("l_pv", offs4)
         l_xt = load_list("l_xt", offs)
@@ -109,7 +109,7 @@ def tile_picked_tokens_bare_two_levelled_one_endsplit_kernel(
         pv = [board("pv0")]
         spread(w2_plane, w2_stage)
         nc.vector.tensor_copy(out=w2_sc[:], in_=w2_plane[:].rearrange("p (m t) -> p t m", t=PACK))
-        pv.extend(board("pv%d" % t) for t in range(1, PACK))
+        pv.extend(board("pv%d" % t) for t in range(1, PACK - 1))
 
         def deal_w2(t0, t1):
             nc.vector.tensor_copy(
@@ -141,6 +141,8 @@ def tile_picked_tokens_bare_two_levelled_one_endsplit_kernel(
         make_b(0, words, scales, (0, FIRST))
         deal_w2(1, PACK)
         for t in range(1, PACK):
+            if t == PACK - 1:
+                pv.append(board("pv%d" % t, "w2_raw"))
             make_b(t, words, scales, (0, FIRST))
         for a, b in ((FIRST, J // 2), (J // 2, J)):
             words, scales = gather_notes(a, b)
@@ -165,7 +167,7 @@ def tile_picked_tokens_bare_two_levelled_one_endsplit_kernel(
             product(w_d[:, t, :].bitcast(FP4X4), w_sc[:, t, :], xt_g[:].bitcast(FP8X4), xt_gs[:], acc[:])
             nc.vector.tensor_copy(out=a_sb[t][:], in_=acc[:])
 
-        pw = [board("pw0", "w2_raw")]
+        pw = [board("pw0", "xo_g", nc.gpsimd)]
         make_a(0)
         pw.append(board("pw1", "w_plane", nc.gpsimd))
         make_a(1)
@@ -202,7 +204,7 @@ def tile_picked_tokens_bare_two_levelled_one_endsplit_kernel(
                 nc.vector.reciprocal(out=level[:, col], in_=inv_level[:, col])
         nc.vector.reciprocal(out=late[:, 1:], in_=inv_level[:, 1:])
 
-        planes = [tile("planes0", [P, PACK, O // 2], BF16, "a_sb3"), tile("planes1", [P, PACK, O // 2], BF16, "w2_raw")]
+        planes = [tile("planes0", [P, PACK, O // 2], BF16, "a_sb3"), tile("planes1", [P, PACK, O // 2], BF16, "xo_g")]
 
         def fetch(t, half, levels):
             a, b = half * O // 2, (half + 1) * O // 2

from contextlib import ExitStack

import concourse.mybir as mybir

F32 = mybir.dt.float32
BF16 = mybir.dt.bfloat16
I32 = mybir.dt.int32
U32 = mybir.dt.uint32
U16 = mybir.dt.uint16
U8 = mybir.dt.uint8
FP8X4 = mybir.dt.float8_e4m3fn_x4
FP4X4 = mybir.dt.float4_e2m1fn_x4
ALU = mybir.AluOpType
COPY = mybir.ActivationFunctionType.Copy
AXIS_X = mybir.AxisListType.X

P = 128
PACK = 4
J, R, T, C, O, N, U = 512, 512, 1024, 1024, 512, 256, 1024
GROUP = 16
FLOPS = 2 * 512 * 512 * 512 * 2 + 2 * 512 * 256 * 512

FIRST = 128


def tile_picked_tokens_bare_two_levelled_one_endsplit_kernel(
    tc, xt_words, xt_scales, w_words, w_scales, xo_words, xo_scales, w2_words, w2_scales,
    sa, wb_words, wb_scales, offs, offs2, offs3, offs4, offs5, offs6, offs7, out,
):
    nc = tc.nc
    with ExitStack() as ctx:
        lists = ctx.enter_context(tc.tile_pool(name="lists", bufs=1))
        sb = ctx.enter_context(tc.tile_pool(name="sb", bufs=1))
        psum = ctx.enter_context(tc.psum_pool(name="psum", bufs=8))

        def tile(name, shape, dtype, tag=None):
            return sb.tile(shape, dtype, name=name, tag=tag or name, align_bytes=64)

        def load_list(name, src):
            t = lists.tile([P, J // GROUP], U16, name=name)
            nc.sync.dma_start(t[:], src)
            return t

        def part(lst, a, b):
            return lst[:, a // GROUP : b // GROUP]

        def zeroed_plane(name, width):
            t = tile(name, [P, width], U8)
            nc.gpsimd.memset(t[:].bitcast(I32), 0)
            return t

        def load_plane(plane, src):
            for q in range(4):
                nc.sync.dma_start(plane[32 * q : 32 * q + 4, :].bitcast(I32), src[0, 4 * q : 4 * q + 4, :].bitcast(I32))

        def load_stage(name, src, width):
            t = tile(name, [4, 4, width // 4], I32)
            nc.sync.dma_start(t[:], src[0].bitcast(I32).rearrange("(q r) w -> r q w", q=4))
            return t

        def spread(plane, stage):
            for q in range(4):
                nc.vector.tensor_copy(out=plane[32 * q : 32 * q + 4, :].bitcast(I32), in_=stage[:, q, :])

        def load_words(name, src, width, dtype):
            t = tile(name, [P, width], dtype)
            nc.sync.dma_start(t[:].bitcast(I32), src.bitcast(I32))
            return t

        def board(name, tag=None, engine=nc.vector):
            t = tile(name, [P, C], F32, tag)
            engine.memset(t[:], 0.0)
            return t

        def product(lhs, lhs_scale, rhs, rhs_scale, acc):
            nc.tensor.matmul_mx(out=acc, lhsT=lhs, lhsT_scale=lhs_scale, rhs=rhs, rhs_scale=rhs_scale, start=True, stop=True)

        def scatter(window, lst, values, a, b):
            nc.scalar.activation(out=window[:].indirect(part(lst, a, b)), in_=values[:, a:b], func=COPY)

        xo_plane = zeroed_plane("xo_plane", T)
        w2_plane = zeroed_plane("w2_plane", R)
        xt_plane = zeroed_plane("xt_plane", T)
        w_plane = zeroed_plane("w_plane", R)
        wb_plane = zeroed_plane("wb_plane", N)
        w2_stage = load_stage("w2_stage", w2_scales, R)
        l_xo = load_list("l_xo", offs2)
        xo_win = load_words("xo_win", xo_words[0], T, U16)
        load_plane(xo_plane, xo_scales)
        w2_raw = load_words("w2_raw", w2_words[0].rearrange("p n t -> p (n t)"), R, U32)
        l_pv = load_list("l_pv", offs4)
        l_xt = load_list("l_xt", offs)
        xt_win = load_words("xt_win", xt_words[0].rearrange("p n t -> p (n t)"), T, U32)
        load_plane(xt_plane, xt_scales)
        w_raw = load_words("w_raw", w_words[0], 2 * R, U8)
        load_plane(w_plane, w_scales)
        l_pw = load_list("l_pw", offs3)
        sa_sb = tile("sa_sb", [P, PACK], F32)
        nc.sync.dma_start(sa_sb[:], sa.rearrange("(p t) o -> p (t o)", t=PACK))
        l_hid = load_list("l_hid", offs5)
        wb = load_words("wb", wb_words[0].rearrange("p n t -> p (n t)"), N, U32)
        load_plane(wb_plane, wb_scales)
        l_m2 = load_list("l_m2", offs6)
        l_m3 = load_list("l_m3", offs7)

        w2_sc = tile("w2_sc", [P, PACK, P], U8)
        w2_d = tile("w2_d", [P, PACK, P], U32)
        b_sb = [tile("b_sb%d" % t, [P, J], F32) for t in range(PACK)]
        pv = [board("pv0")]
        spread(w2_plane, w2_stage)
        nc.vector.tensor_copy(out=w2_sc[:], in_=w2_plane[:].rearrange("p (m t) -> p t m", t=PACK))
        pv.extend(board("pv%d" % t) for t in range(1, PACK - 1))

        def deal_w2(t0, t1):
            nc.vector.tensor_copy(
                out=w2_d[:, t0:t1, :].rearrange("p t m -> p m t"),
                in_=w2_raw[:].rearrange("p (m t) -> p m t", t=PACK)[:, :, t0:t1],
            )

        def gather_notes(a, b):
            words = tile("xo_g%d" % a, [P, b - a], U16, "xo_g")
            scales = tile("xo_gs%d" % a, [P, b - a], U8, "xo_gs")
            nc.vector.tensor_copy(out=scales[:], in_=xo_plane[:].indirect(part(l_xo, a, b)))
            nc.vector.tensor_copy(out=words[:], in_=xo_win[:].indirect(part(l_xo, a, b)))
            return words, scales

        def make_b(t, words, scales, cuts):
            acc = psum.tile([P, J], F32, name="acc")
            a, b = cuts[0], cuts[-1]
            for c, d in zip(cuts, cuts[1:]):
                cols = slice(c - a, d - a)
                product(w2_d[:, t, :].bitcast(FP8X4), w2_sc[:, t, :], words[:, cols].bitcast(FP4X4), scales[:, cols], acc[:, c:d])
            if (t, a) == (0, 0):
                nc.scalar.activation(out=b_sb[t][:, a:b], in_=acc[:, a:b], func=COPY)
            else:
                nc.vector.tensor_copy(out=b_sb[t][:, a:b], in_=acc[:, a:b])
            scatter(pv[t], l_pv, b_sb[t], a, b)

        words, scales = gather_notes(0, FIRST)
        deal_w2(0, 1)
        make_b(0, words, scales, (0, FIRST))
        deal_w2(1, PACK)
        for t in range(1, PACK):
            if t == PACK - 1:
                pv.append(board("pv%d" % t, "w2_raw"))
            make_b(t, words, scales, (0, FIRST))
        for a, b in ((FIRST, J // 2), (J // 2, J)):
            words, scales = gather_notes(a, b)
            for t in range(PACK):
                make_b(t, words, scales, (a, b))

        xt_g = tile("xt_g", [P, J], U32, "xo_win")
        xt_gs = tile("xt_gs", [P, J], U8, "xo_plane")
        nc.vector.tensor_copy(out=xt_g[:], in_=xt_win[:].indirect(l_xt[:]))
        nc.vector.tensor_copy(out=xt_gs[:], in_=xt_plane[:].indirect(l_xt[:]))
        w_sc = tile("w_sc", [P, PACK, P], U8, "w2_sc")
        w_d = tile("w_d", [P, PACK, 2 * P], U8, "w2_d")
        nc.vector.tensor_copy(
            out=w_d[:].rearrange("p t (m e) -> p t m e", e=2),
            in_=w_raw[:].rearrange("p (m t e) -> p t m e", t=PACK, e=2),
        )
        nc.vector.tensor_copy(out=w_sc[:], in_=w_plane[:].rearrange("p (m t) -> p t m", t=PACK))
        a_sb = [tile("a_sb%d" % t, [P, J], F32) for t in range(PACK)]

        def make_a(t):
            acc = psum.tile([P, J], F32, name="acc")
            product(w_d[:, t, :].bitcast(FP4X4), w_sc[:, t, :], xt_g[:].bitcast(FP8X4), xt_gs[:], acc[:])
            nc.vector.tensor_copy(out=a_sb[t][:], in_=acc[:])

        pw = [board("pw0", "xo_g", nc.gpsimd)]
        make_a(0)
        pw.append(board("pw1", "w_plane", nc.gpsimd))
        make_a(1)
        make_a(2)
        make_a(3)
        inv_sa = tile("inv_sa", [P, PACK], F32, "xt_plane")
        nc.vector.reciprocal(out=inv_sa[:], in_=sa_sb[:])
        m2 = [board("m2_0", "xo_win", nc.gpsimd), board("m2_1", "xo_plane", nc.gpsimd)]
        m3 = [board("m3_0", "w2_d", nc.gpsimd), board("m3_1", "w2_sc", nc.gpsimd)]
        inv_weight = tile("inv_weight", [P, PACK], F32)
        nc.vector.tensor_scalar(out=inv_weight[:], in0=inv_sa[:], scalar1=1.0 / C, scalar2=None, op0=ALU.mult)
        pg = []
        inv_level = tile("inv_level", [P, PACK], F32)
        level = tile("level", [P, PACK], F32)
        late = tile("late", [P, PACK], F32)
        halves = (slice(0, C // 2), slice(C // 2, C))

        for t in range(PACK):
            col = slice(t, t + 1)
            scatter(pw[t % 2], l_pw, a_sb[t], 0, J)
            pg.append(tile("pg%d" % t, [P, C], F32, "sums%d" % (t - 1) if t else None))
            for cols in halves:
                nc.vector.tensor_tensor(out=pg[t][:, cols], in0=pw[t % 2][:, cols], in1=pv[t][:, cols], op=ALU.max)
            sums = tile("sums%d" % t, [P, 2], F32)
            for h, cols in enumerate(halves):
                nc.vector.tensor_reduce(
                    out=sums[:, h : h + 1], in_=pg[t][:, cols], axis=AXIS_X, op=ALU.add, apply_absolute_value=True
                )
            nc.vector.tensor_scalar(
                out=inv_level[:, col], in0=sums[:, 0:1], scalar1=sums[:, 1:2], scalar2=inv_weight[:, col],
                op0=ALU.add, op1=ALU.mult,
            )
            if t < PACK - 1:
                nc.vector.reciprocal(out=level[:, col], in_=inv_level[:, col])
        nc.vector.reciprocal(out=late[:, 1:], in_=inv_level[:, 1:])

        planes = [tile("planes0", [P, PACK, O // 2], BF16, "a_sb3"), tile("planes1", [P, PACK, O // 2], BF16, "xo_g")]

        def fetch(t, half, levels):
            a, b = half * O // 2, (half + 1) * O // 2
            nc.scalar.activation(
                out=planes[half][:, t, :], in_=pg[t][:].indirect(part(l_hid, a, b)), func=COPY, scale=levels[:, t : t + 1]
            )

        for t in range(PACK - 1):
            fetch(t, 0, level)
        fetch(0, 1, level)
        fetch(PACK - 1, 0, late)
        for t in range(1, PACK):
            fetch(t, 1, late)

        m0 = [tile("m0_%d" % n, [P, O], F32) for n in range(2)]
        m1 = [tile("m1_%d" % n, [P, O], F32) for n in range(2)]

        def weave(dst, src):
            nc.vector.tensor_copy(
                out=dst.rearrange("p (c i) t -> p c t i", i=4), in_=src.rearrange("p t (c i) -> p c t i", i=4)
            )

        def quantise(woven, a, b):
            words = tile("hid_q%d" % a, [P, b - a], U32)
            scales = tile("hid_s%d" % a, [P, b - a], U8)
            nc.vector.quantize_mx(out=words[:].bitcast(FP8X4), scales=scales[:], in_=woven[:].rearrange("p c t -> p (c t)"))
            return words, scales

        def make_p(n, words, scales, cuts):
            acc = psum.tile([P, O], F32, name="acc")
            rows = slice(n * P, (n + 1) * P)
            for c, d in zip(cuts, cuts[1:]):
                cols = slice(c - cuts[0], d - cuts[0])
                product(wb[:, rows].bitcast(FP8X4), wb_plane[:, rows], words[:, cols].bitcast(FP8X4), scales[:, cols], acc[:, c:d])
            return acc

        def split(n, acc, a, b):
            nc.vector.tensor_scalar(out=m0[n][:, a:b], in0=acc[:, a:b], scalar1=0.0, scalar2=None, op0=ALU.max)
            scatter(m2[n], l_m2, m0[n], a, b)
            nc.vector.tensor_scalar(out=m1[n][:, a:b], in0=acc[:, a:b], scalar1=-1.0, scalar2=0.0, op0=ALU.mult, op1=ALU.max)
            scatter(m3[n], l_m3, m1[n], a, b)

        def store(n, pieces):
            res = tile("res%d" % n, [P, U], F32)
            width = U // pieces
            for u in range(0, U, width):
                cols = slice(u, u + width)
                nc.vector.tensor_tensor(out=res[:, cols], in0=m2[n][:, cols], in1=m3[n][:, cols], op=ALU.subtract)
                nc.sync.dma_start(out[n * P : (n + 1) * P, cols], res[:, cols])

        held_by = None
        for a, b in ((0, FIRST), (FIRST, O // 2), (O // 2, O)):
            half, start = divmod(a, O // 2)
            woven = tile("woven%d" % a, [P, b - a, PACK], BF16, held_by)
            weave(woven[:], planes[half][:, :, start : start + b - a])
            words, scales = quantise(woven, a, b)
            held_by = "hid_q%d" % a
            for n in range(2):
                split(n, make_p(n, words, scales, (a, b)), a, b)
        store(0, 2)
        store(1, 4)
